import numpy as np
import ml_dtypes


def mxq(x, axis, fmt="e4m3"):
    dtype, down = {"e4m3": (ml_dtypes.float8_e4m3fn, 7), "e5m2": (ml_dtypes.float8_e5m2, 14)}[fmt]
    v = np.moveaxis(np.asarray(x, np.float32).astype(ml_dtypes.bfloat16).astype(np.float64), axis, -1)
    blocks = v.reshape(v.shape[:-1] + (-1, 32))
    amax = np.abs(blocks).max(-1, keepdims=True)
    byte = np.maximum(np.where(amax > 0, np.frexp(amax)[1] - 1 + 127, 0) - down, 1)
    scale = np.exp2(byte - 127.0)
    codes = (blocks / scale).astype(np.float32).astype(dtype).astype(np.float64)
    return np.moveaxis((codes * scale).reshape(v.shape), -1, axis)


WIDE = False


def mx_kscale(k):
    if not WIDE:
        return np.ones(k)
    levels = np.array([10, -10, 5, -5, 0])
    if k % 512:
        return np.exp2(np.random.permutation(np.resize(levels, k // 32))).repeat(32)
    a = np.empty((k // 512, 16))
    for p in range(k // 512):
        a[p, :8] = np.random.permutation(np.resize(levels, 8))
        for g in range(8):
            far = levels[np.abs(levels - a[p, g]) >= 10]
            a[p, g + 8] = far[np.random.randint(len(far))]
    return np.exp2(a.ravel()).repeat(32)


def f64(x):
    return np.asarray(x).astype(np.float64)


def striped(idx):
    return np.tile(idx.reshape(-1, 16).T, (8, 1)).astype(np.uint16)


def unstriped(offs):
    return offs[:16].T.reshape(-1).astype(np.int64)


E2M1 = np.array([0.0, 0.5, 1.0, 1.5, 2.0, 3.0, 4.0, 6.0, -0.0, -0.5, -1.0, -1.5, -2.0, -3.0, -4.0, -6.0])


def pack_weight(w, fmt):
    k, n = w.shape
    w = f64(np.asarray(w, np.float32).astype(ml_dtypes.bfloat16)).reshape(k // 32, 32, n)
    amax = np.abs(w).max(1)
    if fmt == "e4m3":
        byte = np.frexp(amax)[1] - 1 + 127 - 7
    else:
        mant, ex = np.frexp(amax / 6.0)
        byte = np.where(mant > 0.5, ex, ex - 1) + 127
    byte = np.clip(np.where(amax > 0, byte, 1), 1, 254)
    scaled = (w * np.exp2(127.0 - byte)[:, None, :]).reshape(k, n).astype(np.float32)
    by_word = np.ascontiguousarray(scaled.reshape(k // 512, 128, 4, n).transpose(0, 1, 3, 2))
    if fmt == "e4m3":
        words = by_word.astype(ml_dtypes.float8_e4m3fn).view(np.uint8)
    else:
        c = by_word.astype(ml_dtypes.float4_e2m1fn).view(np.uint8) & 0xF
        words = (c[..., 0::2] | (c[..., 1::2] << 4)).reshape(k // 512, 128, 2 * n)
    return np.ascontiguousarray(words), np.ascontiguousarray(byte.astype(np.uint8).reshape(k // 512, 16, n))


def unpack_weight(words, scales, fmt):
    g, _, n = scales.shape
    words = np.ascontiguousarray(words).reshape(g, 128, n, -1)
    if fmt == "e4m3":
        vals = words.view(ml_dtypes.float8_e4m3fn).astype(np.float64)
    else:
        nib = np.empty((g, 128, n, 4), np.uint8)
        nib[..., 0::2] = words & 0xF
        nib[..., 1::2] = words >> 4
        vals = E2M1[nib]
    vals = vals * np.repeat(np.exp2(scales.astype(np.float64) - 127.0), 8, axis=1)[..., None]
    return vals.transpose(0, 1, 3, 2).reshape(g * 512, n)


def gelu(v):
    return 0.5 * v * (1.0 + np.tanh(np.sqrt(2.0 / np.pi) * (v + 0.044715 * v**3)))


def striped8(idx):
    return np.concatenate([v.reshape(-1, 16).T for v in idx]).astype(np.uint16)


def unstriped8(offs):
    return np.stack([offs[16 * g:16 * g + 16].T.reshape(-1) for g in range(8)]).astype(np.int64)


def runs(v, idx8):
    k = np.arange(v.shape[0])
    return v[k[:, None], idx8[k % 512 // 64]]


def bf(x):
    return np.asarray(x, np.float32).astype(ml_dtypes.bfloat16)


def planes(Y):
    n, m = Y.shape
    b = f64(bf(Y)).reshape(n // 32, 32, m)
    amax = np.abs(b).max(1)
    byte = np.clip(np.where(amax > 0, np.frexp(amax)[1] - 1 + 127 - 7, 1), 1, 254)
    codes = (b * np.exp2(127.0 - byte)[:, None, :]).reshape(n, m).astype(np.float32).astype(ml_dtypes.float8_e4m3fn).view(np.uint8)
    words = codes.reshape(n // 512, 128, 4, m).transpose(0, 1, 3, 2)
    return np.ascontiguousarray(words), np.ascontiguousarray(byte.astype(np.uint8).reshape(n // 512, 16, m))


K, H, N, T, S, P = 1536, 512, 1024, 2048, 1024, 512


def setup_inputs():
    n = np.random.standard_normal
    s = mx_kscale(K)[:, None]
    u = mx_kscale(H)[:, None]
    d = {}
    d["tab_words"], d["tab_scales"] = pack_weight(n((K, T)) * s, "e4m3")
    d["offs"] = striped8(np.stack([np.random.permutation(T)[:S] for _ in range(8)]))
    d["pos1"] = striped(np.random.permutation(S)[:P])
    d["pos2"] = striped(np.random.permutation(S)[:P])
    d["w1"] = (1.6 * n((K, H)) / s / K ** 0.5).astype(np.float32)
    d["w2_words"], d["w2_scales"] = pack_weight(n((K, H)) / s / K ** 0.5, "e2m1")
    d["gain"] = (u[:, 0] * np.exp(0.3 * n(H))).astype(np.float32)
    d["w3"] = (n((H, N)) / u / H ** 0.5 * np.exp(0.8 * n(N))).astype(np.float32)
    return d


def reference(tab_words, tab_scales, offs, pos1, pos2, w1, w2_words, w2_scales, gain, w3):
    v = runs(unpack_weight(tab_words, tab_scales, "e4m3"), unstriped8(offs))
    a = mxq(f64(w1), 0, "e4m3").T @ v
    b = unpack_weight(w2_words, w2_scales, "e2m1").T @ v
    h = np.minimum(np.tanh(a), b)
    x1 = h[:, unstriped(pos1)]
    x2 = h[:, unstriped(pos2)]
    z = f64(gain)[:, None] * (x1 + x2) / (1.0 + np.square(x1))
    y = mxq(f64(w3), 0, "e4m3").T @ mxq(z, 0, "e4m3")
    words, scales = planes(y)
    return y, words, scales

@@ -1,0 +1,293 @@
+from contextlib import ExitStack
+
+import concourse.mybir as mybir
+
+K, H, N, T, S, M = 1536, 512, 1024, 2048, 1024, 512
+FLOPS = 2 * (2 * K * H * S + H * N * M)
+
+F32 = mybir.dt.float32
+BF16 = mybir.dt.bfloat16
+I32 = mybir.dt.int32
+U32 = mybir.dt.uint32
+U16 = mybir.dt.uint16
+U8 = mybir.dt.uint8
+FP8X4 = mybir.dt.float8_e4m3fn_x4
+FP4X4 = mybir.dt.float4_e2m1fn_x4
+ACT = mybir.ActivationFunctionType
+ALU = mybir.AluOpType
+
+P = 128
+PACK = 4
+PASSES = K // (P * PACK)
+BANK = 512
+HALVES = S // BANK
+GROUPS = N // (P * PACK)
+CHUNK = 128
+CHUNKS = M // CHUNK
+LIST_ROWS = 16
+ROW0 = LIST_ROWS - 2 * PASSES
+
+
+def tile_list_recount_batch_comparator_kernel(
+    tc, tab_words, tab_scales, offs, pos1, pos2, w1, w2_words, w2_scales, gain, w3, out_0, out_1, out_2
+):
+    nc = tc.nc
+    with ExitStack() as ctx:
+        lists = ctx.enter_context(tc.tile_pool(name="lists", bufs=1))
+        keep = ctx.enter_context(tc.tile_pool(name="keep", bufs=1))
+        psum = ctx.enter_context(tc.psum_pool(name="psum", bufs=1))
+
+        def tile(shape, dtype, name, tag=None):
+            return keep.tile(shape, dtype, name=name, tag=tag or name, align_bytes=64)
+
+        offs_sb = lists.tile([P, S // LIST_ROWS], U16, name="offs_sb")
+        pos1_sb = lists.tile([P, M // LIST_ROWS], U16, name="pos1_sb")
+        pos2_sb = lists.tile([P, M // LIST_ROWS], U16, name="pos2_sb")
+
+        tab_rows = tile([P, T], U8, "tab_rows")
+        w2_scale_raw = tile([P, PASSES, H], U8, "w2_scale_raw")
+        v_planes = tile([P, PASSES, S], U8, "v_planes")
+        zero = tile([P, 1], F32, "zero", tag="after_tanh")
+        nc.gpsimd.memset(tab_rows[:].bitcast(I32), 0)
+        for q in range(4):
+            nc.gpsimd.dma_start(
+                out=tab_rows[32 * q + ROW0 : 32 * q + ROW0 + 4 * PASSES, :].bitcast(I32),
+                in_=tab_scales[:, 4 * q : 4 * q + 4, :].rearrange("a r n -> r a n").bitcast(I32),
+            )
+        nc.vector.memset(w2_scale_raw[:].bitcast(I32), 0)
+        nc.vector.memset(v_planes[:].bitcast(I32), 0)
+        nc.vector.memset(zero[:], 0.0)
+
+        tab_sb = [tile([P, T], U32, f"tab{a}") for a in range(PASSES)]
+
+        def load_tab(a):
+            nc.sync.dma_start(
+                out=tab_sb[a][:].bitcast(I32), in_=tab_words[a].rearrange("p n i -> p (n i)").bitcast(I32)
+            )
+
+        nc.sync.dma_start(offs_sb[:], offs)
+        nc.sync.dma_start(pos1_sb[:], pos1)
+        nc.sync.dma_start(pos2_sb[:], pos2)
+        for a in range(PASSES):
+            load_tab(a)
+        w2_raw = tile([P, PASSES, 2 * H], U8, "w2_raw")
+        nc.sync.dma_start(out=w2_raw[:].bitcast(I32), in_=w2_words.rearrange("a p c -> p a c").bitcast(I32))
+        w1_raw = [tile([P, PACK, H], F32, f"w1_raw{a}") for a in range(PASSES)]
+        for a in range(PASSES):
+            rows = w1[a * P * PACK : (a + 1) * P * PACK, :]
+            nc.sync.dma_start(out=w1_raw[a][:], in_=rows.rearrange("(p j) c -> p j c", j=PACK))
+        w3_raw = tile([P, PACK, N], F32, "w3_raw")
+        w3_rows = w3.rearrange("(i t u) n -> t i u n", t=PACK, u=PACK)
+        for t in range(PACK):
+            nc.sync.dma_start(out=w3_raw[:, t, :], in_=w3_rows[t])
+        gain_sb = tile([P, PACK], F32, "gain_sb")
+        gain_rows = gain.rearrange("(i t u) -> u i t", t=PACK, u=PACK)
+        with nc.allow_non_contiguous_dma(reason="one gain value for each channel of a partition"):
+            for u in range(PACK):
+                nc.sync.dma_start(out=gain_sb[u:P:PACK, :], in_=gain_rows[u])
+
+        for q in range(4):
+            nc.gpsimd.dma_start(
+                out=w2_scale_raw[32 * q : 32 * q + 4, :, :].bitcast(I32),
+                in_=w2_scales[:, 4 * q : 4 * q + 4, :].rearrange("a r c -> r a c").bitcast(I32),
+            )
+
+        picked_rows = tile([P, S], U8, "picked_rows")
+        nc.vector.tensor_copy(picked_rows[:], tab_rows[:].indirect(offs_sb[:]))
+        for q in range(4):
+            nc.gpsimd.dma_start(
+                out=v_planes[32 * q : 32 * q + 4, :, :].bitcast(I32),
+                in_=picked_rows[32 * q + ROW0 : 32 * q + ROW0 + 4 * PASSES, :].bitcast(I32),
+            )
+        v_codes = [tile([P, S], U32, f"v_codes{a}") for a in range(PASSES)]
+        for a in range(PASSES):
+            nc.vector.tensor_copy(v_codes[a][:], tab_sb[a][:].indirect(offs_sb[:]))
+
+        w2_codes = tile([P, PASSES, PACK, 2 * P], U8, "w2_codes")
+        w2_planes = tile([P, PASSES, PACK, P], U8, "w2_planes")
+        nc.vector.tensor_copy(
+            out=w2_codes[:].bitcast(I32).rearrange("p a t (i w) -> p a t i w", w=2),
+            in_=w2_raw[:].bitcast(I32).rearrange("p a (i t w) -> p a t i w", t=PACK, w=2),
+        )
+        nc.vector.tensor_copy(
+            out=w2_planes[:].bitcast(I32),
+            in_=w2_scale_raw[:].bitcast(I32).rearrange("p a (i t) -> p a t i", t=PACK),
+        )
+
+        w1_codes = [[tile([P, P], U32, f"w1_codes{a}_{t}") for t in range(PACK)] for a in range(PASSES)]
+        w1_planes = [[tile([P, P], U8, f"w1_planes{a}_{t}") for t in range(PACK)] for a in range(PASSES)]
+        for a in range(PASSES):
+            for t in range(PACK):
+                grouped = tile([P, P * PACK], BF16, f"w1_bf{a}_{t}")
+                nc.scalar.activation(
+                    out=grouped[:].rearrange("p (i u j) -> p i j u", u=PACK, j=PACK),
+                    in_=w1_raw[a][:].rearrange("p j (i t u) -> p t i j u", t=PACK, u=PACK)[:, t],
+                    func=ACT.Copy,
+                )
+                nc.vector.quantize_mx(
+                    out=w1_codes[a][t][:].bitcast(FP8X4), scales=w1_planes[a][t][:], in_=grouped[:]
+                )
+
+        def bank(kind, t, half):
+            name = f"{kind}{t % 2}{half}"
+            return psum.tile([P, BANK], F32, name=name, tag=name)
+
+        def pass_a(acc, t, half, a):
+            cols = slice(half * BANK, (half + 1) * BANK)
+            nc.tensor.matmul_mx(
+                out=acc[:], lhsT=w1_codes[a][t][:].bitcast(FP8X4), lhsT_scale=w1_planes[a][t][:],
+                rhs=v_codes[a][:, cols].bitcast(FP8X4), rhs_scale=v_planes[:, a, cols],
+                start=(a == 0), stop=(a == PASSES - 1),
+            )
+
+        def pass_b(acc, t, half, a):
+            cols = slice(half * BANK, (half + 1) * BANK)
+            nc.tensor.matmul_mx(
+                out=acc[:], lhsT=w2_codes[:, a, t, :].bitcast(FP4X4), lhsT_scale=w2_planes[:, a, t, :],
+                rhs=v_codes[a][:, cols].bitcast(FP8X4), rhs_scale=v_planes[:, a, cols],
+                start=(a == 0), stop=(a == PASSES - 1),
+            )
+
+        acc_a, acc_b, bounded = {}, {}, {}
+        h = [tile([P, S], F32, f"h{t}") for t in range(PACK)]
+        x1 = tile([P, PACK, M], F32, "x1")
+        total = tile([P, PACK, M], F32, "total")
+        square = tile([P, PACK, M], F32, "square")
+
+        def do_tanh(t):
+            for half in range(HALVES):
+                bounded[t, half] = tile([P, BANK], F32, f"bounded{t}{half}")
+                nc.scalar.activation(out=bounded[t, half][:], in_=acc_a[t, half][:], func=ACT.Tanh, bias=zero[:])
+
+        def do_min(t):
+            for half in range(HALVES):
+                nc.vector.tensor_tensor(
+                    h[t][:, half * BANK : (half + 1) * BANK], acc_b[t, half][:], bounded[t, half][:], ALU.min
+                )
+            nc.vector.tensor_copy(x1[:, t, :], h[t][:].indirect(pos1_sb[:]))
+
+        def do_square(t, cols):
+            nc.scalar.activation(out=square[:, t, cols], in_=x1[:, t, cols], func=ACT.Square)
+
+        def do_factor(t, cols):
+            nc.scalar.activation(out=factor[:, t, cols], in_=square[:, t, cols], func=ACT.Abs_reciprocal_sqrt, bias=1.0)
+            nc.scalar.activation(out=square[:, t, cols], in_=factor[:, t, cols], func=ACT.Square)
+            if t < PACK - 1:
+                nc.gpsimd.tensor_scalar(factor[:, t, cols], square[:, t, cols], gain_sb[:, t : t + 1], 0.0, ALU.mult, ALU.add)
+            else:
+                nc.scalar.activation(out=factor[:, t, cols], in_=square[:, t, cols], func=ACT.Copy, scale=gain_sb[:, t : t + 1])
+
+        def add_x2(t, lo, hi):
+            nc.vector.tensor_tensor(
+                total[:, t, lo:hi], h[t][:].indirect(pos2_sb[:, lo // LIST_ROWS : hi // LIST_ROWS]), x1[:, t, lo:hi], ALU.add
+            )
+
+        first = [(t, half) for t in (0, 1) for half in range(HALVES)]
+        for key in first:
+            acc_a[key] = bank("a", *key)
+            acc_b[key] = bank("b", *key)
+        for a in range(PASSES):
+            for key in first:
+                pass_b(acc_b[key], *key, a)
+            for key in first:
+                pass_a(acc_a[key], *key, a)
+        do_tanh(0)
+        do_tanh(1)
+        for t in (2, 3):
+            for half in range(HALVES):
+                acc_a[t, half] = bank("a", t, half)
+                for a in range(PASSES):
+                    pass_a(acc_a[t, half], t, half, a)
+            do_tanh(t)
+        whole = slice(0, M)
+        for t in (0, 1):
+            do_min(t)
+            do_square(t, whole)
+        factor = tile([P, PACK, M], F32, "factor", tag="after_tanh")
+        for t in (0, 1):
+            do_factor(t, whole)
+        for t in (2, 3):
+            for half in range(HALVES):
+                acc_b[t, half] = bank("b", t, half)
+                for a in range(PASSES):
+                    pass_b(acc_b[t, half], t, half, a)
+        add_x2(0, 0, M)
+
+        w3_codes = [tile([P, P * PACK], U32, f"w3_codes{g}") for g in range(GROUPS)]
+        w3_planes = [tile([P, P * PACK], U8, f"w3_planes{g}") for g in range(GROUPS)]
+        w3_bf = [tile([P, P * PACK * PACK], BF16, f"w3_bf{g}", tag=f"bounded{g}0") for g in range(GROUPS)]
+        for g in range(GROUPS):
+            for part in range(2):
+                qs = slice(part * P // 2, (part + 1) * P // 2)
+                nc.scalar.activation(
+                    out=w3_bf[g][:].rearrange("p (t q j) -> p q j t", t=PACK, j=PACK)[:, qs],
+                    in_=w3_raw[:].rearrange("p j (g q t) -> p g q j t", g=GROUPS, t=PACK)[:, g, qs],
+                    func=ACT.Copy,
+                )
+
+        do_min(2)
+        do_square(2, whole)
+        do_factor(2, whole)
+        do_min(3)
+        for lo in range(0, M, M // 2):
+            do_square(3, slice(lo, lo + M // 2))
+            do_factor(3, slice(lo, lo + M // 2))
+        for g in range(GROUPS):
+            nc.vector.quantize_mx(out=w3_codes[g][:].bitcast(FP8X4), scales=w3_planes[g][:], in_=w3_bf[g][:])
+
+        add_x2(1, 0, M)
+        add_x2(2, 0, M)
+
+        y_planes = tile([P, GROUPS, M], U8, "y_planes")
+        out_rows = out_0.rearrange("(g p t) m -> g p t m", p=P, t=PACK)
+        out_words = out_1.rearrange("g p m t -> p g (m t)").bitcast(I32)
+        z_codes, z_planes = {}, {}
+
+        def make_z(c):
+            cols = slice(c * CHUNK, (c + 1) * CHUNK)
+            add_x2(PACK - 1, cols.start, cols.stop)
+            z_bf = tile([P, CHUNK * PACK], BF16, f"z_bf{c}")
+            nc.vector.tensor_tensor(
+                z_bf[:].rearrange("p (n i t) -> p n t i", i=2, t=PACK),
+                total[:, :, cols].rearrange("p t (n i) -> p n t i", i=2),
+                factor[:, :, cols].rearrange("p t (n i) -> p n t i", i=2),
+                ALU.mult,
+            )
+            z_codes[c] = tile([P, CHUNK], U32, f"z_codes{c}")
+            z_planes[c] = tile([P, CHUNK], U8, f"z_planes{c}")
+            nc.vector.quantize_mx(out=z_codes[c][:].bitcast(FP8X4), scales=z_planes[c][:], in_=z_bf[:])
+
+        def make_y(c):
+            cols = slice(c * CHUNK, (c + 1) * CHUNK)
+            y_codes = tile([P, GROUPS, CHUNK], U32, f"y_codes{c}")
+            for g in range(GROUPS):
+                acc = bank("a", c, g)
+                for t in range(PACK):
+                    nc.tensor.matmul_mx(
+                        out=acc[:, t * CHUNK : (t + 1) * CHUNK],
+                        lhsT=w3_codes[g][:, t * P : (t + 1) * P].bitcast(FP8X4),
+                        lhsT_scale=w3_planes[g][:, t * P : (t + 1) * P],
+                        rhs=z_codes[c][:].bitcast(FP8X4), rhs_scale=z_planes[c][:],
+                        start=True, stop=True,
+                    )
+                y = tile([P, PACK * CHUNK], F32, f"y{c}{g}")
+                nc.scalar.copy(out=y[:], in_=acc[:])
+                nc.sync.dma_start(out=out_rows[g][:, :, cols], in_=y[:].rearrange("p (t m) -> p t m", t=PACK))
+                y_bf = tile([P, CHUNK * PACK], BF16, f"y_bf{c}{g}")
+                nc.vector.tensor_copy(
+                    out=y_bf[:].rearrange("p (n i t) -> p n t i", i=2, t=PACK),
+                    in_=y[:].rearrange("p (t n i) -> p n t i", i=2, t=PACK),
+                )
+                nc.vector.quantize_mx(out=y_codes[:, g, :].bitcast(FP8X4), scales=y_planes[:, g, cols], in_=y_bf[:])
+            nc.sync.dma_start(out=out_words[:, :, cols], in_=y_codes[:].bitcast(I32))
+
+        make_z(0)
+        for c in range(CHUNKS):
+            if c + 1 < CHUNKS:
+                make_z(c + 1)
+            make_y(c)
+        for q in range(4):
+            nc.sync.dma_start(
+                out=out_2[:, 4 * q : 4 * q + 4, :].rearrange("g r m -> r g m").bitcast(I32),
+                in_=y_planes[32 * q : 32 * q + 4, :, :].bitcast(I32),
+            )

@@ -49,14 +49,10 @@ def tile_list_recount_batch_comparator_kernel(
         v_planes = tile([P, PASSES, S], U8, "v_planes")
         zero = tile([P, 1], F32, "zero", tag="after_tanh")
         nc.gpsimd.memset(tab_rows[:].bitcast(I32), 0)
-        for q in range(4):
-            nc.gpsimd.dma_start(
-                out=tab_rows[32 * q + ROW0 : 32 * q + ROW0 + 4 * PASSES, :].bitcast(I32),
-                in_=tab_scales[:, 4 * q : 4 * q + 4, :].rearrange("a r n -> r a n").bitcast(I32),
-            )
         nc.vector.memset(w2_scale_raw[:].bitcast(I32), 0)
         nc.vector.memset(v_planes[:].bitcast(I32), 0)
         nc.vector.memset(zero[:], 0.0)
+        small_queues = (nc.scalar, nc.scalar, nc.sync, nc.sync)
 
         tab_sb = [tile([P, T], U32, f"tab{a}") for a in range(PASSES)]
 
@@ -65,27 +61,21 @@ def tile_list_recount_batch_comparator_kernel(
                 out=tab_sb[a][:].bitcast(I32), in_=tab_words[a].rearrange("p n i -> p (n i)").bitcast(I32)
             )
 
+        def load_w1(a, dest):
+            rows = w1[a * P * PACK : (a + 1) * P * PACK, :]
+            nc.sync.dma_start(out=dest, in_=rows.rearrange("(p j) c -> p j c", j=PACK))
+
         nc.sync.dma_start(offs_sb[:], offs)
-        nc.sync.dma_start(pos1_sb[:], pos1)
-        nc.sync.dma_start(pos2_sb[:], pos2)
-        for a in range(PASSES):
-            load_tab(a)
+        load_tab(0)
+        for q in range(4):
+            small_queues[q].dma_start(
+                out=tab_rows[32 * q + ROW0 : 32 * q + ROW0 + 4 * PASSES, :].bitcast(I32),
+                in_=tab_scales[:, 4 * q : 4 * q + 4, :].rearrange("a r n -> r a n").bitcast(I32),
+            )
         w2_raw = tile([P, PASSES, 2 * H], U8, "w2_raw")
         nc.sync.dma_start(out=w2_raw[:].bitcast(I32), in_=w2_words.rearrange("a p c -> p a c").bitcast(I32))
-        w1_raw = [tile([P, PACK, H], F32, f"w1_raw{a}") for a in range(PASSES)]
-        for a in range(PASSES):
-            rows = w1[a * P * PACK : (a + 1) * P * PACK, :]
-            nc.sync.dma_start(out=w1_raw[a][:], in_=rows.rearrange("(p j) c -> p j c", j=PACK))
-        w3_raw = tile([P, PACK, N], F32, "w3_raw")
-        w3_rows = w3.rearrange("(i t u) n -> t i u n", t=PACK, u=PACK)
-        for t in range(PACK):
-            nc.sync.dma_start(out=w3_raw[:, t, :], in_=w3_rows[t])
-        gain_sb = tile([P, PACK], F32, "gain_sb")
-        gain_rows = gain.rearrange("(i t u) -> u i t", t=PACK, u=PACK)
-        with nc.allow_non_contiguous_dma(reason="one gain value for each channel of a partition"):
-            for u in range(PACK):
-                nc.sync.dma_start(out=gain_sb[u:P:PACK, :], in_=gain_rows[u])
-
+        for a in range(1, PASSES):
+            load_tab(a)
         for q in range(4):
             nc.gpsimd.dma_start(
                 out=w2_scale_raw[32 * q : 32 * q + 4, :, :].bitcast(I32),
@@ -95,16 +85,31 @@ def tile_list_recount_batch_comparator_kernel(
         picked_rows = tile([P, S], U8, "picked_rows")
         nc.vector.tensor_copy(picked_rows[:], tab_rows[:].indirect(offs_sb[:]))
         for q in range(4):
-            nc.gpsimd.dma_start(
+            small_queues[q].dma_start(
                 out=v_planes[32 * q : 32 * q + 4, :, :].bitcast(I32),
                 in_=picked_rows[32 * q + ROW0 : 32 * q + ROW0 + 4 * PASSES, :].bitcast(I32),
             )
-        v_codes = [tile([P, S], U32, f"v_codes{a}") for a in range(PASSES)]
+        w1_raw = [tile([P, PACK, H], F32, f"w1_raw{a}") for a in range(PASSES)]
+        for a in range(PASSES):
+            load_w1(a, w1_raw[a][:])
+        nc.sync.dma_start(pos1_sb[:], pos1)
+        nc.sync.dma_start(pos2_sb[:], pos2)
+        v_codes = [tile([P, S], U32, f"v_codes{a}", tag="tab_rows" if a == 0 else None) for a in range(PASSES)]
         for a in range(PASSES):
             nc.vector.tensor_copy(v_codes[a][:], tab_sb[a][:].indirect(offs_sb[:]))
 
+        w3_raw = tile([P, PACK, N], F32, "w3_raw")
+        gain_sb = tile([P, PACK], F32, "gain_sb")
+        w3_rows = w3.rearrange("(i t u) n -> t i u n", t=PACK, u=PACK)
+        for t in range(PACK):
+            nc.sync.dma_start(out=w3_raw[:, t, :], in_=w3_rows[t])
+        gain_rows = gain.rearrange("(i t u) -> u i t", t=PACK, u=PACK)
+        with nc.allow_non_contiguous_dma(reason="one gain value for each channel of a partition"):
+            for u in range(PACK):
+                nc.gpsimd.dma_start(out=gain_sb[u:P:PACK, :], in_=gain_rows[u])
+
         w2_codes = tile([P, PASSES, PACK, 2 * P], U8, "w2_codes")
-        w2_planes = tile([P, PASSES, PACK, P], U8, "w2_planes")
+        w2_planes = tile([P, PASSES, PACK, P], U8, "w2_planes", tag="tab0")
         nc.vector.tensor_copy(
             out=w2_codes[:].bitcast(I32).rearrange("p a t (i w) -> p a t i w", w=2),
             in_=w2_raw[:].bitcast(I32).rearrange("p a (i t w) -> p a t i w", t=PACK, w=2),

@@ -82,20 +82,23 @@ def tile_list_recount_batch_comparator_kernel(
                 in_=w2_scales[:, 4 * q : 4 * q + 4, :].rearrange("a r c -> r a c").bitcast(I32),
             )
 
-        picked_rows = tile([P, S], U8, "picked_rows")
+        v_codes = [tile([P, S], U32, "v_codes0")]
+        nc.vector.tensor_copy(v_codes[0][:], tab_sb[0][:].indirect(offs_sb[:]))
+        picked_rows = tile([P, S], U8, "picked_rows", tag="tab0")
         nc.vector.tensor_copy(picked_rows[:], tab_rows[:].indirect(offs_sb[:]))
+        w1_raw = [tile([P, PACK, H], F32, f"w1_raw{a}") for a in range(PASSES)]
+        load_w1(0, w1_raw[0][:])
         for q in range(4):
             small_queues[q].dma_start(
                 out=v_planes[32 * q : 32 * q + 4, :, :].bitcast(I32),
                 in_=picked_rows[32 * q + ROW0 : 32 * q + ROW0 + 4 * PASSES, :].bitcast(I32),
             )
-        w1_raw = [tile([P, PACK, H], F32, f"w1_raw{a}") for a in range(PASSES)]
-        for a in range(PASSES):
+        for a in range(1, PASSES):
             load_w1(a, w1_raw[a][:])
         nc.sync.dma_start(pos1_sb[:], pos1)
         nc.sync.dma_start(pos2_sb[:], pos2)
-        v_codes = [tile([P, S], U32, f"v_codes{a}", tag="tab_rows" if a == 0 else None) for a in range(PASSES)]
-        for a in range(PASSES):
+        for a in range(1, PASSES):
+            v_codes.append(tile([P, S], U32, f"v_codes{a}", tag="tab_rows" if a == 1 else None))
             nc.vector.tensor_copy(v_codes[a][:], tab_sb[a][:].indirect(offs_sb[:]))
 
         w3_raw = tile([P, PACK, N], F32, "w3_raw")
@@ -106,31 +109,35 @@ def tile_list_recount_batch_comparator_kernel(
         gain_rows = gain.rearrange("(i t u) -> u i t", t=PACK, u=PACK)
         with nc.allow_non_contiguous_dma(reason="one gain value for each channel of a partition"):
             for u in range(PACK):
-                nc.gpsimd.dma_start(out=gain_sb[u:P:PACK, :], in_=gain_rows[u])
+                nc.sync.dma_start(out=gain_sb[u:P:PACK, :], in_=gain_rows[u])
 
         w2_codes = tile([P, PASSES, PACK, 2 * P], U8, "w2_codes")
-        w2_planes = tile([P, PASSES, PACK, P], U8, "w2_planes", tag="tab0")
-        nc.vector.tensor_copy(
+        w2_planes = tile([P, PASSES, PACK, P], U8, "w2_planes")
+        nc.gpsimd.tensor_copy(
             out=w2_codes[:].bitcast(I32).rearrange("p a t (i w) -> p a t i w", w=2),
             in_=w2_raw[:].bitcast(I32).rearrange("p a (i t w) -> p a t i w", t=PACK, w=2),
         )
-        nc.vector.tensor_copy(
+        nc.gpsimd.tensor_copy(
             out=w2_planes[:].bitcast(I32),
             in_=w2_scale_raw[:].bitcast(I32).rearrange("p a (i t) -> p a t i", t=PACK),
         )
 
-        w1_codes = [[tile([P, P], U32, f"w1_codes{a}_{t}") for t in range(PACK)] for a in range(PASSES)]
-        w1_planes = [[tile([P, P], U8, f"w1_planes{a}_{t}") for t in range(PACK)] for a in range(PASSES)]
+        w1_codes = [tile([P, H], U32, f"w1_codes{a}") for a in range(PASSES)]
+        w1_planes = [tile([P, H], U8, f"w1_planes{a}") for a in range(PASSES)]
         for a in range(PASSES):
+            grouped = tile([P, PACK, P * PACK], BF16, f"w1_bf{a}")
             for t in range(PACK):
-                grouped = tile([P, P * PACK], BF16, f"w1_bf{a}_{t}")
                 nc.scalar.activation(
-                    out=grouped[:].rearrange("p (i u j) -> p i j u", u=PACK, j=PACK),
+                    out=grouped[:, t, :].rearrange("p (i u j) -> p i j u", u=PACK, j=PACK),
                     in_=w1_raw[a][:].rearrange("p j (i t u) -> p t i j u", t=PACK, u=PACK)[:, t],
                     func=ACT.Copy,
                 )
+            step = 1 if a == PASSES - 1 else PACK
+            for t in range(0, PACK, step):
                 nc.vector.quantize_mx(
-                    out=w1_codes[a][t][:].bitcast(FP8X4), scales=w1_planes[a][t][:], in_=grouped[:]
+                    out=w1_codes[a][:, t * P : (t + step) * P].bitcast(FP8X4),
+                    scales=w1_planes[a][:, t * P : (t + step) * P],
+                    in_=grouped[:, t : t + step, :].rearrange("p t c -> p (t c)"),
                 )
 
         def bank(kind, t, half):
@@ -140,7 +147,8 @@ def tile_list_recount_batch_comparator_kernel(
         def pass_a(acc, t, half, a):
             cols = slice(half * BANK, (half + 1) * BANK)
             nc.tensor.matmul_mx(
-                out=acc[:], lhsT=w1_codes[a][t][:].bitcast(FP8X4), lhsT_scale=w1_planes[a][t][:],
+                out=acc[:], lhsT=w1_codes[a][:, t * P : (t + 1) * P].bitcast(FP8X4),
+                lhsT_scale=w1_planes[a][:, t * P : (t + 1) * P],
                 rhs=v_codes[a][:, cols].bitcast(FP8X4), rhs_scale=v_planes[:, a, cols],
                 start=(a == 0), stop=(a == PASSES - 1),
             )

from contextlib import ExitStack

import concourse.mybir as mybir

K, H, N, T, S, M = 1536, 512, 1024, 2048, 1024, 512
FLOPS = 2 * (2 * K * H * S + H * N * M)

F32 = mybir.dt.float32
BF16 = mybir.dt.bfloat16
I32 = mybir.dt.int32
U32 = mybir.dt.uint32
U16 = mybir.dt.uint16
U8 = mybir.dt.uint8
FP8X4 = mybir.dt.float8_e4m3fn_x4
FP4X4 = mybir.dt.float4_e2m1fn_x4
ACT = mybir.ActivationFunctionType
ALU = mybir.AluOpType

P = 128
PACK = 4
PASSES = K // (P * PACK)
BANK = 512
HALVES = S // BANK
GROUPS = N // (P * PACK)
CHUNK = 128
CHUNKS = M // CHUNK
LIST_ROWS = 16
ROW0 = LIST_ROWS - 2 * PASSES


def tile_list_recount_batch_comparator_kernel(
    tc, tab_words, tab_scales, offs, pos1, pos2, w1, w2_words, w2_scales, gain, w3, out_0, out_1, out_2
):
    nc = tc.nc
    with ExitStack() as ctx:
        lists = ctx.enter_context(tc.tile_pool(name="lists", bufs=1))
        keep = ctx.enter_context(tc.tile_pool(name="keep", bufs=1))
        psum = ctx.enter_context(tc.psum_pool(name="psum", bufs=1))

        def tile(shape, dtype, name, tag=None):
            return keep.tile(shape, dtype, name=name, tag=tag or name, align_bytes=64)

        offs_sb = lists.tile([P, S // LIST_ROWS], U16, name="offs_sb")
        pos1_sb = lists.tile([P, M // LIST_ROWS], U16, name="pos1_sb")
        pos2_sb = lists.tile([P, M // LIST_ROWS], U16, name="pos2_sb")

        tab_rows = tile([P, T], U8, "tab_rows")
        w2_scale_raw = tile([P, PASSES, H], U8, "w2_scale_raw")
        v_planes = tile([P, PASSES, S], U8, "v_planes")
        zero = tile([P, 1], F32, "zero", tag="after_tanh")
        nc.gpsimd.memset(tab_rows[:].bitcast(I32), 0)
        nc.vector.memset(w2_scale_raw[:].bitcast(I32), 0)
        nc.vector.memset(v_planes[:].bitcast(I32), 0)
        nc.vector.memset(zero[:], 0.0)
        small_queues = (nc.scalar, nc.scalar, nc.sync, nc.sync)

        tab_sb = [tile([P, T], U32, f"tab{a}") for a in range(PASSES)]

        def load_tab(a):
            nc.sync.dma_start(
                out=tab_sb[a][:].bitcast(I32), in_=tab_words[a].rearrange("p n i -> p (n i)").bitcast(I32)
            )

        def load_w1(a, dest):
            rows = w1[a * P * PACK : (a + 1) * P * PACK, :]
            nc.sync.dma_start(out=dest, in_=rows.rearrange("(p j) c -> p j c", j=PACK))

        nc.sync.dma_start(offs_sb[:], offs)
        load_tab(0)
        for q in range(4):
            small_queues[q].dma_start(
                out=tab_rows[32 * q + ROW0 : 32 * q + ROW0 + 4 * PASSES, :].bitcast(I32),
                in_=tab_scales[:, 4 * q : 4 * q + 4, :].rearrange("a r n -> r a n").bitcast(I32),
            )
        w2_raw = tile([P, PASSES, 2 * H], U8, "w2_raw")
        nc.sync.dma_start(out=w2_raw[:].bitcast(I32), in_=w2_words.rearrange("a p c -> p a c").bitcast(I32))
        for a in range(1, PASSES):
            load_tab(a)
        for q in range(4):
            nc.gpsimd.dma_start(
                out=w2_scale_raw[32 * q : 32 * q + 4, :, :].bitcast(I32),
                in_=w2_scales[:, 4 * q : 4 * q + 4, :].rearrange("a r c -> r a c").bitcast(I32),
            )

        v_codes = [tile([P, S], U32, "v_codes0")]
        nc.vector.tensor_copy(v_codes[0][:], tab_sb[0][:].indirect(offs_sb[:]))
        picked_rows = tile([P, S], U8, "picked_rows", tag="tab0")
        nc.vector.tensor_copy(picked_rows[:], tab_rows[:].indirect(offs_sb[:]))
        w1_raw = [tile([P, PACK, H], F32, f"w1_raw{a}") for a in range(PASSES)]
        load_w1(0, w1_raw[0][:])
        for q in range(4):
            small_queues[q].dma_start(
                out=v_planes[32 * q : 32 * q + 4, :, :].bitcast(I32),
                in_=picked_rows[32 * q + ROW0 : 32 * q + ROW0 + 4 * PASSES, :].bitcast(I32),
            )
        for a in range(1, PASSES):
            load_w1(a, w1_raw[a][:])
        nc.sync.dma_start(pos1_sb[:], pos1)
        nc.sync.dma_start(pos2_sb[:], pos2)
        for a in range(1, PASSES):
            v_codes.append(tile([P, S], U32, f"v_codes{a}", tag="tab_rows" if a == 1 else None))
            nc.vector.tensor_copy(v_codes[a][:], tab_sb[a][:].indirect(offs_sb[:]))

        w3_raw = tile([P, PACK, N], F32, "w3_raw")
        gain_sb = tile([P, PACK], F32, "gain_sb")
        w3_rows = w3.rearrange("(i t u) n -> t i u n", t=PACK, u=PACK)
        for t in range(PACK):
            nc.sync.dma_start(out=w3_raw[:, t, :], in_=w3_rows[t])
        gain_rows = gain.rearrange("(i t u) -> u i t", t=PACK, u=PACK)
        with nc.allow_non_contiguous_dma(reason="one gain value for each channel of a partition"):
            for u in range(PACK):
                nc.sync.dma_start(out=gain_sb[u:P:PACK, :], in_=gain_rows[u])

        w2_codes = tile([P, PASSES, PACK, 2 * P], U8, "w2_codes")
        w2_planes = tile([P, PASSES, PACK, P], U8, "w2_planes")
        nc.gpsimd.tensor_copy(
            out=w2_codes[:].bitcast(I32).rearrange("p a t (i w) -> p a t i w", w=2),
            in_=w2_raw[:].bitcast(I32).rearrange("p a (i t w) -> p a t i w", t=PACK, w=2),
        )
        nc.gpsimd.tensor_copy(
            out=w2_planes[:].bitcast(I32),
            in_=w2_scale_raw[:].bitcast(I32).rearrange("p a (i t) -> p a t i", t=PACK),
        )

        w1_codes = [tile([P, H], U32, f"w1_codes{a}") for a in range(PASSES)]
        w1_planes = [tile([P, H], U8, f"w1_planes{a}") for a in range(PASSES)]
        for a in range(PASSES):
            grouped = tile([P, PACK, P * PACK], BF16, f"w1_bf{a}")
            for t in range(PACK):
                nc.scalar.activation(
                    out=grouped[:, t, :].rearrange("p (i u j) -> p i j u", u=PACK, j=PACK),
                    in_=w1_raw[a][:].rearrange("p j (i t u) -> p t i j u", t=PACK, u=PACK)[:, t],
                    func=ACT.Copy,
                )
            step = 1 if a == PASSES - 1 else PACK
            for t in range(0, PACK, step):
                nc.vector.quantize_mx(
                    out=w1_codes[a][:, t * P : (t + step) * P].bitcast(FP8X4),
                    scales=w1_planes[a][:, t * P : (t + step) * P],
                    in_=grouped[:, t : t + step, :].rearrange("p t c -> p (t c)"),
                )

        def bank(kind, t, half):
            name = f"{kind}{t % 2}{half}"
            return psum.tile([P, BANK], F32, name=name, tag=name)

        def pass_a(acc, t, half, a):
            cols = slice(half * BANK, (half + 1) * BANK)
            nc.tensor.matmul_mx(
                out=acc[:], lhsT=w1_codes[a][:, t * P : (t + 1) * P].bitcast(FP8X4),
                lhsT_scale=w1_planes[a][:, t * P : (t + 1) * P],
                rhs=v_codes[a][:, cols].bitcast(FP8X4), rhs_scale=v_planes[:, a, cols],
                start=(a == 0), stop=(a == PASSES - 1),
            )

        def pass_b(acc, t, half, a):
            cols = slice(half * BANK, (half + 1) * BANK)
            nc.tensor.matmul_mx(
                out=acc[:], lhsT=w2_codes[:, a, t, :].bitcast(FP4X4), lhsT_scale=w2_planes[:, a, t, :],
                rhs=v_codes[a][:, cols].bitcast(FP8X4), rhs_scale=v_planes[:, a, cols],
                start=(a == 0), stop=(a == PASSES - 1),
            )

        acc_a, acc_b, bounded = {}, {}, {}
        h = [tile([P, S], F32, f"h{t}") for t in range(PACK)]
        x1 = tile([P, PACK, M], F32, "x1")
        total = tile([P, PACK, M], F32, "total")
        square = tile([P, PACK, M], F32, "square")

        def do_tanh(t):
            for half in range(HALVES):
                bounded[t, half] = tile([P, BANK], F32, f"bounded{t}{half}")
                nc.scalar.activation(out=bounded[t, half][:], in_=acc_a[t, half][:], func=ACT.Tanh, bias=zero[:])

        def do_min(t):
            for half in range(HALVES):
                nc.vector.tensor_tensor(
                    h[t][:, half * BANK : (half + 1) * BANK], acc_b[t, half][:], bounded[t, half][:], ALU.min
                )
            nc.vector.tensor_copy(x1[:, t, :], h[t][:].indirect(pos1_sb[:]))

        def do_square(t, cols):
            nc.scalar.activation(out=square[:, t, cols], in_=x1[:, t, cols], func=ACT.Square)

        def do_factor(t, cols):
            nc.scalar.activation(out=factor[:, t, cols], in_=square[:, t, cols], func=ACT.Abs_reciprocal_sqrt, bias=1.0)
            nc.scalar.activation(out=square[:, t, cols], in_=factor[:, t, cols], func=ACT.Square)
            if t < PACK - 1:
                nc.gpsimd.tensor_scalar(factor[:, t, cols], square[:, t, cols], gain_sb[:, t : t + 1], 0.0, ALU.mult, ALU.add)
            else:
                nc.scalar.activation(out=factor[:, t, cols], in_=square[:, t, cols], func=ACT.Copy, scale=gain_sb[:, t : t + 1])

        def add_x2(t, lo, hi):
            nc.vector.tensor_tensor(
                total[:, t, lo:hi], h[t][:].indirect(pos2_sb[:, lo // LIST_ROWS : hi // LIST_ROWS]), x1[:, t, lo:hi], ALU.add
            )

        first = [(t, half) for t in (0, 1) for half in range(HALVES)]
        for key in first:
            acc_a[key] = bank("a", *key)
            acc_b[key] = bank("b", *key)
        for a in range(PASSES):
            for key in first:
                pass_b(acc_b[key], *key, a)
            for key in first:
                pass_a(acc_a[key], *key, a)
        do_tanh(0)
        do_tanh(1)
        for t in (2, 3):
            for half in range(HALVES):
                acc_a[t, half] = bank("a", t, half)
                for a in range(PASSES):
                    pass_a(acc_a[t, half], t, half, a)
            do_tanh(t)
        whole = slice(0, M)
        for t in (0, 1):
            do_min(t)
            do_square(t, whole)
        factor = tile([P, PACK, M], F32, "factor", tag="after_tanh")
        for t in (0, 1):
            do_factor(t, whole)
        for t in (2, 3):
            for half in range(HALVES):
                acc_b[t, half] = bank("b", t, half)
                for a in range(PASSES):
                    pass_b(acc_b[t, half], t, half, a)
        add_x2(0, 0, M)

        w3_codes = [tile([P, P * PACK], U32, f"w3_codes{g}") for g in range(GROUPS)]
        w3_planes = [tile([P, P * PACK], U8, f"w3_planes{g}") for g in range(GROUPS)]
        w3_bf = [tile([P, P * PACK * PACK], BF16, f"w3_bf{g}", tag=f"bounded{g}0") for g in range(GROUPS)]
        for g in range(GROUPS):
            for part in range(2):
                qs = slice(part * P // 2, (part + 1) * P // 2)
                nc.scalar.activation(
                    out=w3_bf[g][:].rearrange("p (t q j) -> p q j t", t=PACK, j=PACK)[:, qs],
                    in_=w3_raw[:].rearrange("p j (g q t) -> p g q j t", g=GROUPS, t=PACK)[:, g, qs],
                    func=ACT.Copy,
                )

        do_min(2)
        do_square(2, whole)
        do_factor(2, whole)
        do_min(3)
        for lo in range(0, M, M // 2):
            do_square(3, slice(lo, lo + M // 2))
            do_factor(3, slice(lo, lo + M // 2))
        for g in range(GROUPS):
            nc.vector.quantize_mx(out=w3_codes[g][:].bitcast(FP8X4), scales=w3_planes[g][:], in_=w3_bf[g][:])

        add_x2(1, 0, M)
        add_x2(2, 0, M)

        y_planes = tile([P, GROUPS, M], U8, "y_planes")
        out_rows = out_0.rearrange("(g p t) m -> g p t m", p=P, t=PACK)
        out_words = out_1.rearrange("g p m t -> p g (m t)").bitcast(I32)
        z_codes, z_planes = {}, {}

        def make_z(c):
            cols = slice(c * CHUNK, (c + 1) * CHUNK)
            add_x2(PACK - 1, cols.start, cols.stop)
            z_bf = tile([P, CHUNK * PACK], BF16, f"z_bf{c}")
            nc.vector.tensor_tensor(
                z_bf[:].rearrange("p (n i t) -> p n t i", i=2, t=PACK),
                total[:, :, cols].rearrange("p t (n i) -> p n t i", i=2),
                factor[:, :, cols].rearrange("p t (n i) -> p n t i", i=2),
                ALU.mult,
            )
            z_codes[c] = tile([P, CHUNK], U32, f"z_codes{c}")
            z_planes[c] = tile([P, CHUNK], U8, f"z_planes{c}")
            nc.vector.quantize_mx(out=z_codes[c][:].bitcast(FP8X4), scales=z_planes[c][:], in_=z_bf[:])

        def make_y(c):
            cols = slice(c * CHUNK, (c + 1) * CHUNK)
            y_codes = tile([P, GROUPS, CHUNK], U32, f"y_codes{c}")
            for g in range(GROUPS):
                acc = bank("a", c, g)
                for t in range(PACK):
                    nc.tensor.matmul_mx(
                        out=acc[:, t * CHUNK : (t + 1) * CHUNK],
                        lhsT=w3_codes[g][:, t * P : (t + 1) * P].bitcast(FP8X4),
                        lhsT_scale=w3_planes[g][:, t * P : (t + 1) * P],
                        rhs=z_codes[c][:].bitcast(FP8X4), rhs_scale=z_planes[c][:],
                        start=True, stop=True,
                    )
                y = tile([P, PACK * CHUNK], F32, f"y{c}{g}")
                nc.scalar.copy(out=y[:], in_=acc[:])
                nc.sync.dma_start(out=out_rows[g][:, :, cols], in_=y[:].rearrange("p (t m) -> p t m", t=PACK))
                y_bf = tile([P, CHUNK * PACK], BF16, f"y_bf{c}{g}")
                nc.vector.tensor_copy(
                    out=y_bf[:].rearrange("p (n i t) -> p n t i", i=2, t=PACK),
                    in_=y[:].rearrange("p (t n i) -> p n t i", i=2, t=PACK),
                )
                nc.vector.quantize_mx(out=y_codes[:, g, :].bitcast(FP8X4), scales=y_planes[:, g, cols], in_=y_bf[:])
            nc.sync.dma_start(out=out_words[:, :, cols], in_=y_codes[:].bitcast(I32))

        make_z(0)
        for c in range(CHUNKS):
            if c + 1 < CHUNKS:
                make_z(c + 1)
            make_y(c)
        for q in range(4):
            nc.sync.dma_start(
                out=out_2[:, 4 * q : 4 * q + 4, :].rearrange("g r m -> r g m").bitcast(I32),
                in_=y_planes[32 * q : 32 * q + 4, :, :].bitcast(I32),
            )
